import numpy as np
import ml_dtypes


def mxq(x, axis, fmt="e4m3"):
    dtype, down = {"e4m3": (ml_dtypes.float8_e4m3fn, 7), "e5m2": (ml_dtypes.float8_e5m2, 14)}[fmt]
    v = np.moveaxis(np.asarray(x, np.float32).astype(ml_dtypes.bfloat16).astype(np.float64), axis, -1)
    blocks = v.reshape(v.shape[:-1] + (-1, 32))
    amax = np.abs(blocks).max(-1, keepdims=True)
    byte = np.maximum(np.where(amax > 0, np.frexp(amax)[1] - 1 + 127, 0) - down, 1)
    scale = np.exp2(byte - 127.0)
    codes = (blocks / scale).astype(np.float32).astype(dtype).astype(np.float64)
    return np.moveaxis((codes * scale).reshape(v.shape), -1, axis)


WIDE = False


def mx_kscale(k):
    if not WIDE:
        return np.ones(k)
    levels = np.array([10, -10, 5, -5, 0])
    if k % 512:
        return np.exp2(np.random.permutation(np.resize(levels, k // 32))).repeat(32)
    a = np.empty((k // 512, 16))
    for p in range(k // 512):
        a[p, :8] = np.random.permutation(np.resize(levels, 8))
        for g in range(8):
            far = levels[np.abs(levels - a[p, g]) >= 10]
            a[p, g + 8] = far[np.random.randint(len(far))]
    return np.exp2(a.ravel()).repeat(32)


def f64(x):
    return np.asarray(x).astype(np.float64)


def striped(idx):
    return np.tile(idx.reshape(-1, 16).T, (8, 1)).astype(np.uint16)


def unstriped(offs):
    return offs[:16].T.reshape(-1).astype(np.int64)


K, T, E, C, N = 512, 512, 8, 256, 512
TOP = 4
M = 384


def by_expert(wq, xq):
    return np.concatenate([wq[e].T @ xq[:, e * C:(e + 1) * C] for e in range(E)], axis=1)


def setup_inputs():
    n = np.random.standard_normal
    s = mx_kscale(K)[:, None]
    v = mx_kscale(N)
    deal = np.repeat(np.arange(E), C).reshape(TOP, T)[:, np.random.permutation(T)]
    deal = np.take_along_axis(deal, np.argsort(np.random.rand(TOP, T), axis=0), axis=0)
    for _ in range(8):
        s_, t_ = np.random.permutation(T).reshape(2, -1); r = np.random.randint(TOP, size=T // 2); x, y = deal[r, s_].copy(), deal[r, t_].copy()
        ok = ~((deal[:, s_] == y).any(0) | (deal[:, t_] == x).any(0)); deal[r[ok], s_[ok]] = y[ok]; deal[r[ok], t_[ok]] = x[ok]
    order = np.lexsort((np.random.rand(TOP * T), deal.reshape(-1)))
    slot_token = order % T; pos = np.empty(TOP * T, np.int64); pos[order] = np.arange(TOP * T); pos = pos.reshape(TOP, T)
    g = np.random.uniform(0.5, 1.5, (TOP, T)); g = g / g.sum(0)
    return {
        "xT": (n((K, T)) * s).astype(np.float32),
        "w": (n((E, K, N)) / np.sqrt(K) / s[None] * v[None, None, :]).astype(np.float32),
        "wp": (n((N, M)) / np.sqrt(N) / v[:, None]).astype(np.float32),
        "gate": np.stack([np.tile(r, (N, 1)) for r in g]).astype(np.float32),
        "offs": striped(slot_token),
        "pos1": striped(pos[0]),
        "pos2": striped(pos[1]),
        "pos3": striped(pos[2]),
        "pos4": striped(pos[3]),
    }


def reference(xT, w, wp, gate, offs, pos1, pos2, pos3, pos4):
    idx = unstriped(offs)
    xq = mxq(f64(xT)[:, idx], 0, "e4m3")
    y = by_expert(mxq(f64(w), 1, "e4m3"), xq)
    c = f64(gate[0]) * y[:, unstriped(pos1)] + f64(gate[1]) * y[:, unstriped(pos2)] + f64(gate[2]) * y[:, unstriped(pos3)] + f64(gate[3]) * y[:, unstriped(pos4)]
    return mxq(f64(wp), 0, "e4m3").T @ mxq(c, 0, "e4m3")

@@ -1,0 +1,240 @@
+from contextlib import ExitStack
+
+import concourse.mybir as mybir
+from concourse.masks import make_identity
+
+K, T, E, C, N, M = 512, 512, 8, 256, 512, 384
+TOP = 4
+SLOTS = E * C
+FLOPS = 2 * K * N * SLOTS + 2 * N * M * T
+
+F32 = mybir.dt.float32
+BF16 = mybir.dt.bfloat16
+I32 = mybir.dt.int32
+U32 = mybir.dt.uint32
+U16 = mybir.dt.uint16
+U8 = mybir.dt.uint8
+FP8X4 = mybir.dt.float8_e4m3fn_x4
+MULT = mybir.AluOpType.mult
+
+P = 128
+PACK = 4
+PAIR = 2 * C
+PAIRS = E // 2
+WINDOW = 1408
+RUN = 1024
+LIST_COL = 16
+TOKEN_CHUNKS = ((0, 256), (256, 384), (384, 512))
+
+
+def interleave(engine_copy, dst, src):
+    engine_copy(
+        out=dst.rearrange("p (c i) t -> p c t i", i=4),
+        in_=src.rearrange("p t (c i) -> p c t i", i=4),
+    )
+
+
+def tile_moe_nxt_lin_none_kernel(tc, xT, w, wp, gate, offs, pos1, pos2, pos3, pos4, out):
+    nc = tc.nc
+    with ExitStack() as ctx:
+        keep = ctx.enter_context(tc.tile_pool(name="keep", bufs=1))
+        psum = ctx.enter_context(tc.psum_pool(name="psum", bufs=1))
+
+        def quantize(codes, scales, grouped):
+            nc.vector.quantize_mx(out=codes.bitcast(FP8X4), scales=scales, in_=grouped)
+
+        x_rows = xT.rearrange("(p j) t -> p j t", j=PACK)
+        x_raw = []
+        for h in range(2):
+            t = keep.tile([P, PACK, 256], F32, name=f"x_raw{h}")
+            nc.sync.dma_start(out=t[:], in_=x_rows[:, :, 256 * h : 256 * (h + 1)])
+            x_raw.append(t)
+        offs_sb = keep.tile([P, SLOTS // LIST_COL], U16, name="offs_sb")
+        nc.sync.dma_start(offs_sb[:], offs)
+
+        def load_w(e, c0, c1):
+            t = keep.tile([P, PACK, c1 - c0], F32, name=f"w_raw{e}_{c0}", tag=f"w_raw{e}_{c0}", align_bytes=64)
+            nc.sync.dma_start(out=t[:], in_=w[e].rearrange("(p j) n -> p j n", j=PACK)[:, :, c0:c1])
+            return t
+
+        w_lo = [load_w(e, 0, 256) for e in range(E)]
+        pos_sb = []
+        for r, pos in enumerate((pos1, pos2, pos3, pos4)):
+            t = keep.tile([P, T // LIST_COL], U16, name=f"pos_sb{r}")
+            nc.sync.dma_start(t[:], pos)
+            pos_sb.append(t)
+        gate_sb = keep.tile([P, TOP, T], F32, name="gate_sb")
+        nc.sync.dma_start(out=gate_sb[:], in_=gate[:, 0:P, :].rearrange("r p t -> p r t"))
+        w_t2 = [load_w(e, 256, 384) for e in range(E)]
+        w_t3 = [load_w(e, 384, 512) for e in range(E)]
+        wp_raw = keep.tile([P, PACK, M], F32, name="wp_raw")
+        nc.sync.dma_start(out=wp_raw[:], in_=wp.rearrange("(p j) f -> p j f", j=PACK))
+
+        ident = keep.tile([P, P], F32, name="ident")
+        x_codes = keep.tile([P, WINDOW], U32, name="x_codes", align_bytes=64)
+        x_scales = keep.tile([P, WINDOW], U8, name="x_scales", align_bytes=64)
+        nc.gpsimd.memset(x_scales[:], 0)
+        nc.gpsimd.memset(x_codes[:, T:WINDOW].bitcast(I32), 0)
+        make_identity(nc, ident[:])
+
+        x_bf = [keep.tile([P, 256, PACK], BF16, name=f"x_bf{h}", align_bytes=64) for h in range(2)]
+        interleave(nc.vector.tensor_copy, x_bf[0][:], x_raw[0][:])
+        quantize(x_codes[:, 0:256], x_scales[:, 0:256], x_bf[0][:].rearrange("p c t -> p (c t)"))
+        interleave(nc.scalar.copy, x_bf[1][:, 0:128, :], x_raw[1][:, :, 0:128])
+        interleave(nc.vector.tensor_copy, x_bf[1][:, 128:256, :], x_raw[1][:, :, 128:256])
+        quantize(x_codes[:, 256:512], x_scales[:, 256:512], x_bf[1][:].rearrange("p c t -> p (c t)"))
+
+        y = {}
+        slot_codes, slot_scales = [], []
+
+        def gather_tokens(i):
+            lst = offs_sb[:, i * RUN // LIST_COL : (i + 1) * RUN // LIST_COL]
+            cw = keep.tile([P, RUN], U32, name=f"slot_codes{i}", align_bytes=64)
+            cs = keep.tile([P, RUN], U8, name=f"slot_scales{i}", align_bytes=64)
+            nc.vector.tensor_copy(cw[:], x_codes[:].indirect(lst))
+            nc.vector.tensor_copy(cs[:], x_scales[:].indirect(lst))
+            for h in range(RUN // PAIR):
+                slot_codes.append(cw[:, PAIR * h : PAIR * (h + 1)])
+                slot_scales.append(cs[:, PAIR * h : PAIR * (h + 1)])
+
+        wq = {}
+
+        def quant_w(j, e0, g, n):
+            cw = keep.tile([P, n * P], U32, name=f"w_codes{j}_{e0}", align_bytes=64)
+            cs = keep.tile([P, n * P], U8, name=f"w_scales{j}_{e0}", align_bytes=64)
+            quantize(cw[:], cs[:], g[:].rearrange("p s c t -> p (s c t)"))
+            for s in range(n):
+                wq[(j, e0 + s)] = (cw[:, P * s : P * (s + 1)], cs[:, P * s : P * (s + 1)])
+
+        def staging(j, e0, n):
+            return keep.tile([P, n, P, PACK], BF16, name=f"w_bf{j}_{e0}", tag=f"w_bf{j}_{e0}", align_bytes=64)
+
+        def experts(j, i):
+            bank = psum.tile([P, PAIR], F32, name="bank", tag="bank", bufs=5)
+            for s in range(2):
+                cw, cs = wq[(j, 2 * i + s)]
+                cols = slice(C * s, C * (s + 1))
+                nc.tensor.matmul_mx(
+                    out=bank[:, cols],
+                    lhsT=cw.bitcast(FP8X4),
+                    lhsT_scale=cs,
+                    rhs=slot_codes[i][:, cols].bitcast(FP8X4),
+                    rhs_scale=slot_scales[i][:, cols],
+                    start=True,
+                    stop=True,
+                )
+            nc.scalar.copy(out=y[j][:, PAIR * i : PAIR * (i + 1)], in_=bank[:])
+
+        def combine(j, a, b, late_tag):
+            early = keep.tile([P, 2, b - a], F32, name=f"prod_early{j}_{a}", align_bytes=64)
+            late = keep.tile([P, 2, b - a], F32, name=f"prod_late{j}_{a}", tag=late_tag, align_bytes=64)
+            prods = [early[:, 0, :], early[:, 1, :], late[:, 0, :], late[:, 1, :]]
+            for r in range(TOP):
+                nc.vector.tensor_tensor(
+                    prods[r], y[j][:].indirect(pos_sb[r][:, a // LIST_COL : b // LIST_COL]), gate_sb[:, r, a:b], MULT
+                )
+            nblk = (b - a) // P
+            sums = psum.tile([P, nblk, P], F32, name="sums", tag="sums", bufs=3)
+            for blk in range(nblk):
+                for r in range(TOP):
+                    nc.tensor.matmul(
+                        out=sums[:, blk, :],
+                        lhsT=prods[r][:, P * blk : P * (blk + 1)],
+                        rhs=ident[:],
+                        start=(r == 0),
+                        stop=(r == TOP - 1),
+                        is_transpose=True,
+                    )
+            return sums
+
+        def round_sums(j, a, b, sums):
+            for ci, (ca, cb) in enumerate(TOKEN_CHUNKS):
+                if ca >= a and cb <= b:
+                    src = sums[:, (ca - a) // P : (cb - a) // P, :]
+                    nc.scalar.copy(
+                        out=c_t[ci][:, :, :, 32 * j : 32 * (j + 1), :],
+                        in_=src.rearrange("t b (p u e) -> t b u p e", u=2, e=2),
+                    )
+
+        for i in range(SLOTS // RUN):
+            gather_tokens(i)
+        g1 = staging(1, 0, E)
+        for i in range(PAIRS):
+            g0 = staging(0, 2 * i, 2)
+            for s in range(2):
+                interleave(nc.scalar.copy, g0[:, s], w_lo[2 * i + s][:, :, 0:P])
+                interleave(nc.scalar.copy, g1[:, 2 * i + s], w_lo[2 * i + s][:, :, P : 2 * P])
+            quant_w(0, 2 * i, g0, 2)
+        quant_w(1, 0, g1, E)
+        y[0] = keep.tile([P, SLOTS], F32, name="y0", tag=f"w_raw{E - 1}_0", align_bytes=64)
+        for j in range(1, 4):
+            y[j] = keep.tile([P, SLOTS], F32, name=f"y{j}")
+        for j in range(2):
+            for i in range(PAIRS):
+                experts(j, i)
+        sums0 = combine(0, 0, T, "prod_late0")
+        held = [sums0]
+        for j, raws in ((2, w_t2), (3, w_t3)):
+            g = staging(j, 0, E)
+            for e in range(E):
+                interleave(nc.scalar.copy, g[:, e], raws[e][:])
+            quant_w(j, 0, g, E)
+            for i in range(PAIRS):
+                experts(j, i)
+            held.append(combine(j - 1, 0, T, f"w_bf{j}_0"))
+        c_t = [
+            keep.tile([P, (b - a) // P, 2, P, 2], BF16, name=f"c_t{a}", tag=f"w_raw{E - 3 + ci}_384", align_bytes=64)
+            for ci, (a, b) in enumerate(TOKEN_CHUNKS)
+        ]
+        for j in range(3):
+            round_sums(j, 0, T, held[j])
+
+        wp_bf = keep.tile([P, M, PACK], BF16, name="wp_bf", align_bytes=64)
+        interleave(nc.scalar.copy, wp_bf[:], wp_raw[:])
+        wp_codes = keep.tile([P, M], U32, name="wp_codes", align_bytes=64)
+        wp_scales = keep.tile([P, M], U8, name="wp_scales", align_bytes=64)
+        for f0, f1 in ((0, 256), (256, M)):
+            quantize(wp_codes[:, f0:f1], wp_scales[:, f0:f1], wp_bf[:, f0:f1, :].rearrange("p c t -> p (c t)"))
+
+        out_rows = out.rearrange("(a p) t -> p a t", p=P)
+
+        def project(ci):
+            a, b = TOKEN_CHUNKS[ci]
+            nblk = (b - a) // P
+            words = c_t[ci][:].rearrange("t b u p e -> t (b u p e)").bitcast(F32)
+            back = psum.tile([P, nblk, 2, P], F32, name="back", tag="bank", bufs=5)
+            for blk in range(nblk):
+                for u in range(2):
+                    w0 = (2 * blk + u) * P
+                    nc.tensor.transpose(back[:, blk, u, :], words[:, w0 : w0 + P], ident[:])
+            c_bf = keep.tile([P, (b - a) * PACK], BF16, name=f"c_bf{a}", align_bytes=64)
+            nc.scalar.copy(
+                out=c_bf[:].bitcast(F32).rearrange("p (b t u) -> p b t u", b=nblk, u=2),
+                in_=back[:].rearrange("p b u t -> p b t u"),
+            )
+            c_codes = keep.tile([P, b - a], U32, name=f"c_codes{a}", align_bytes=64)
+            c_scales = keep.tile([P, b - a], U8, name=f"c_scales{a}", align_bytes=64)
+            quantize(c_codes[:], c_scales[:], c_bf[:])
+            res = keep.tile([P, M // P, b - a], F32, name=f"res{a}")
+            per_bank = 512 // (b - a)
+            for f0 in range(0, M // P, per_bank):
+                f1 = min(M // P, f0 + per_bank)
+                acc = psum.tile([P, f1 - f0, b - a], F32, name="acc", tag="bank", bufs=5)
+                for f in range(f0, f1):
+                    nc.tensor.matmul_mx(
+                        out=acc[:, f - f0, :],
+                        lhsT=wp_codes[:, P * f : P * (f + 1)].bitcast(FP8X4),
+                        lhsT_scale=wp_scales[:, P * f : P * (f + 1)],
+                        rhs=c_codes[:].bitcast(FP8X4),
+                        rhs_scale=c_scales[:],
+                        start=True,
+                        stop=True,
+                    )
+                nc.vector.tensor_copy(out=res[:, f0:f1, :], in_=acc[:])
+            nc.sync.dma_start(out=out_rows[:, :, a:b], in_=res[:])
+
+        for ci, (a, b) in enumerate(TOKEN_CHUNKS):
+            round_sums(3, a, b, combine(3, a, b, f"prod_late3_{a}"))
+            if ci > 0:
+                project(ci - 1)
+        project(len(TOKEN_CHUNKS) - 1)

@@ -24,7 +24,8 @@ PAIRS = E // 2
 WINDOW = 1408
 RUN = 1024
 LIST_COL = 16
-TOKEN_CHUNKS = ((0, 256), (256, 384), (384, 512))
+BLOCKS = T // P
+X_PIECES = ((0, 256), (256, 384), (384, 512))
 
 
 def interleave(engine_copy, dst, src):
@@ -45,9 +46,9 @@ def tile_moe_nxt_lin_none_kernel(tc, xT, w, wp, gate, offs, pos1, pos2, pos3, po
 
         x_rows = xT.rearrange("(p j) t -> p j t", j=PACK)
         x_raw = []
-        for h in range(2):
-            t = keep.tile([P, PACK, 256], F32, name=f"x_raw{h}")
-            nc.sync.dma_start(out=t[:], in_=x_rows[:, :, 256 * h : 256 * (h + 1)])
+        for a, b in X_PIECES:
+            t = keep.tile([P, PACK, b - a], F32, name=f"x_raw{a}")
+            nc.sync.dma_start(out=t[:], in_=x_rows[:, :, a:b])
             x_raw.append(t)
         offs_sb = keep.tile([P, SLOTS // LIST_COL], U16, name="offs_sb")
         nc.sync.dma_start(offs_sb[:], offs)
@@ -57,13 +58,16 @@ def tile_moe_nxt_lin_none_kernel(tc, xT, w, wp, gate, offs, pos1, pos2, pos3, po
             nc.sync.dma_start(out=t[:], in_=w[e].rearrange("(p j) n -> p j n", j=PACK)[:, :, c0:c1])
             return t
 
-        w_lo = [load_w(e, 0, 256) for e in range(E)]
+        first = [load_w(0, 0, P), load_w(0, P, 2 * P)]
+        rest = [load_w(e, 0, 2 * P) for e in range(1, E)]
+        w_t0 = [first[0][:]] + [t[:, :, 0:P] for t in rest]
+        w_t1 = [first[1][:]] + [t[:, :, P : 2 * P] for t in rest]
         pos_sb = []
         for r, pos in enumerate((pos1, pos2, pos3, pos4)):
             t = keep.tile([P, T // LIST_COL], U16, name=f"pos_sb{r}")
             nc.sync.dma_start(t[:], pos)
             pos_sb.append(t)
-        gate_sb = keep.tile([P, TOP, T], F32, name="gate_sb")
+        gate_sb = keep.tile([P, TOP, T], F32, name="gate_sb", tag="gate_sb", align_bytes=64)
         nc.sync.dma_start(out=gate_sb[:], in_=gate[:, 0:P, :].rearrange("r p t -> p r t"))
         w_t2 = [load_w(e, 256, 384) for e in range(E)]
         w_t3 = [load_w(e, 384, 512) for e in range(E)]
@@ -73,29 +77,23 @@ def tile_moe_nxt_lin_none_kernel(tc, xT, w, wp, gate, offs, pos1, pos2, pos3, po
         ident = keep.tile([P, P], F32, name="ident")
         x_codes = keep.tile([P, WINDOW], U32, name="x_codes", align_bytes=64)
         x_scales = keep.tile([P, WINDOW], U8, name="x_scales", align_bytes=64)
-        nc.gpsimd.memset(x_scales[:], 0)
-        nc.gpsimd.memset(x_codes[:, T:WINDOW].bitcast(I32), 0)
+        nc.vector.memset(x_scales[:].bitcast(I32), 0)
+        nc.vector.memset(x_codes[:, T:WINDOW].bitcast(I32), 0)
         make_identity(nc, ident[:])
 
-        x_bf = [keep.tile([P, 256, PACK], BF16, name=f"x_bf{h}", align_bytes=64) for h in range(2)]
-        interleave(nc.vector.tensor_copy, x_bf[0][:], x_raw[0][:])
-        quantize(x_codes[:, 0:256], x_scales[:, 0:256], x_bf[0][:].rearrange("p c t -> p (c t)"))
-        interleave(nc.scalar.copy, x_bf[1][:, 0:128, :], x_raw[1][:, :, 0:128])
-        interleave(nc.vector.tensor_copy, x_bf[1][:, 128:256, :], x_raw[1][:, :, 128:256])
-        quantize(x_codes[:, 256:512], x_scales[:, 256:512], x_bf[1][:].rearrange("p c t -> p (c t)"))
+        for (a, b), raw, copy in zip(X_PIECES, x_raw, (nc.vector.tensor_copy, nc.scalar.copy, nc.vector.tensor_copy)):
+            x_bf = keep.tile([P, b - a, PACK], BF16, name=f"x_bf{a}", align_bytes=64)
+            interleave(copy, x_bf[:], raw[:])
+            quantize(x_codes[:, a:b], x_scales[:, a:b], x_bf[:].rearrange("p c t -> p (c t)"))
 
         y = {}
         slot_codes, slot_scales = [], []
 
-        def gather_tokens(i):
+        def gather(window, i, dtype, name, tag):
+            got = keep.tile([P, RUN], dtype, name=name, tag=tag, align_bytes=64)
             lst = offs_sb[:, i * RUN // LIST_COL : (i + 1) * RUN // LIST_COL]
-            cw = keep.tile([P, RUN], U32, name=f"slot_codes{i}", align_bytes=64)
-            cs = keep.tile([P, RUN], U8, name=f"slot_scales{i}", align_bytes=64)
-            nc.vector.tensor_copy(cw[:], x_codes[:].indirect(lst))
-            nc.vector.tensor_copy(cs[:], x_scales[:].indirect(lst))
-            for h in range(RUN // PAIR):
-                slot_codes.append(cw[:, PAIR * h : PAIR * (h + 1)])
-                slot_scales.append(cs[:, PAIR * h : PAIR * (h + 1)])
+            nc.vector.tensor_copy(got[:], window[:].indirect(lst))
+            return [got[:, PAIR * h : PAIR * (h + 1)] for h in range(RUN // PAIR)]
 
         wq = {}
 
@@ -125,21 +123,24 @@ def tile_moe_nxt_lin_none_kernel(tc, xT, w, wp, gate, offs, pos1, pos2, pos3, po
                 )
             nc.scalar.copy(out=y[j][:, PAIR * i : PAIR * (i + 1)], in_=bank[:])
 
-        def combine(j, a, b, late_tag):
-            early = keep.tile([P, 2, b - a], F32, name=f"prod_early{j}_{a}", align_bytes=64)
-            late = keep.tile([P, 2, b - a], F32, name=f"prod_late{j}_{a}", tag=late_tag, align_bytes=64)
-            prods = [early[:, 0, :], early[:, 1, :], late[:, 0, :], late[:, 1, :]]
-            for r in range(TOP):
+        def gated(j, a, b, rs, tag):
+            prod = keep.tile([P, len(rs), b - a], F32, name=f"prod{j}_{a}_{rs[0]}", tag=tag, align_bytes=64)
+            for s, r in enumerate(rs):
                 nc.vector.tensor_tensor(
-                    prods[r], y[j][:].indirect(pos_sb[r][:, a // LIST_COL : b // LIST_COL]), gate_sb[:, r, a:b], MULT
+                    prod[:, s, :],
+                    y[j][:].indirect(pos_sb[r][:, a // LIST_COL : b // LIST_COL]),
+                    gate_sb[:, r, a:b],
+                    MULT,
                 )
-            nblk = (b - a) // P
-            sums = psum.tile([P, nblk, P], F32, name="sums", tag="sums", bufs=3)
-            for blk in range(nblk):
+            return {(r, a // P + blk): prod[:, s, P * blk : P * (blk + 1)] for s, r in enumerate(rs) for blk in range((b - a) // P)}
+
+        def turn_and_add(prods, blocks):
+            sums = psum.tile([P, len(blocks), P], F32, name="sums", tag="sums", bufs=3)
+            for s, blk in enumerate(blocks):
                 for r in range(TOP):
                     nc.tensor.matmul(
-                        out=sums[:, blk, :],
-                        lhsT=prods[r][:, P * blk : P * (blk + 1)],
+                        out=sums[:, s, :],
+                        lhsT=prods[(r, blk)],
                         rhs=ident[:],
                         start=(r == 0),
                         stop=(r == TOP - 1),
@@ -147,24 +148,25 @@ def tile_moe_nxt_lin_none_kernel(tc, xT, w, wp, gate, offs, pos1, pos2, pos3, po
                     )
             return sums
 
-        def round_sums(j, a, b, sums):
-            for ci, (ca, cb) in enumerate(TOKEN_CHUNKS):
-                if ca >= a and cb <= b:
-                    src = sums[:, (ca - a) // P : (cb - a) // P, :]
-                    nc.scalar.copy(
-                        out=c_t[ci][:, :, :, 32 * j : 32 * (j + 1), :],
-                        in_=src.rearrange("t b (p u e) -> t b u p e", u=2, e=2),
-                    )
+        def round_sums(j, blocks, sums):
+            for s, blk in enumerate(blocks):
+                nc.scalar.copy(
+                    out=c_t[blk][:, :, 32 * j : 32 * (j + 1), :],
+                    in_=sums[:, s, :].rearrange("t (p u e) -> t u p e", u=2, e=2),
+                )
 
-        for i in range(SLOTS // RUN):
-            gather_tokens(i)
+        slot_codes += gather(x_codes, 0, U32, "slot_codes0", "slot_codes0")
+        slot_scales += gather(x_scales, 0, U8, "slot_scales0", "slot_scales0")
+        slot_codes += gather(x_codes, 1, U32, "slot_codes1", "slot_codes1")
         g1 = staging(1, 0, E)
         for i in range(PAIRS):
             g0 = staging(0, 2 * i, 2)
             for s in range(2):
-                interleave(nc.scalar.copy, g0[:, s], w_lo[2 * i + s][:, :, 0:P])
-                interleave(nc.scalar.copy, g1[:, 2 * i + s], w_lo[2 * i + s][:, :, P : 2 * P])
+                interleave(nc.scalar.copy, g0[:, s], w_t0[2 * i + s])
+                interleave(nc.scalar.copy, g1[:, 2 * i + s], w_t1[2 * i + s])
             quant_w(0, 2 * i, g0, 2)
+            if i == 1:
+                slot_scales += gather(x_scales, 1, U8, "slot_scales1", "w_bf0_2")
         quant_w(1, 0, g1, E)
         y[0] = keep.tile([P, SLOTS], F32, name="y0", tag=f"w_raw{E - 1}_0", align_bytes=64)
         for j in range(1, 4):
@@ -172,57 +174,70 @@ def tile_moe_nxt_lin_none_kernel(tc, xT, w, wp, gate, offs, pos1, pos2, pos3, po
         for j in range(2):
             for i in range(PAIRS):
                 experts(j, i)
-        sums0 = combine(0, 0, T, "prod_late0")
-        held = [sums0]
-        for j, raws in ((2, w_t2), (3, w_t3)):
+        every = list(range(BLOCKS))
+        held = [turn_and_add(gated(0, 0, T, every, "prod0"), every)]
+
+        def upper(j, raws):
             g = staging(j, 0, E)
             for e in range(E):
                 interleave(nc.scalar.copy, g[:, e], raws[e][:])
             quant_w(j, 0, g, E)
             for i in range(PAIRS):
                 experts(j, i)
-            held.append(combine(j - 1, 0, T, f"w_bf{j}_0"))
+
+        upper(2, w_t2)
+        prods = gated(1, 0, T, [0, 1], "prod1")
+        prods.update(gated(1, 0, T, [2, 3], "w_bf2_0"))
+        held.append(turn_and_add(prods, every))
+        upper(3, w_t3)
+        prods = gated(2, 0, T // 2, every, "prod2")
+        prods.update(gated(2, T // 2, T, every, "w_bf3_0"))
+        held.append(turn_and_add(prods, every))
         c_t = [
-            keep.tile([P, (b - a) // P, 2, P, 2], BF16, name=f"c_t{a}", tag=f"w_raw{E - 3 + ci}_384", align_bytes=64)
-            for ci, (a, b) in enumerate(TOKEN_CHUNKS)
+            keep.tile([P, 2, P, 2], BF16, name=f"c_t{blk}", tag=f"w_raw{E - BLOCKS + blk}_384", align_bytes=64)
+            for blk in range(BLOCKS)
         ]
         for j in range(3):
-            round_sums(j, 0, T, held[j])
+            round_sums(j, every, held[j])
 
-        wp_bf = keep.tile([P, M, PACK], BF16, name="wp_bf", align_bytes=64)
+        wp_bf = keep.tile([P, M, PACK], BF16, name="wp_bf", tag="slot_codes1", align_bytes=64)
         interleave(nc.scalar.copy, wp_bf[:], wp_raw[:])
-        wp_codes = keep.tile([P, M], U32, name="wp_codes", align_bytes=64)
+
+        c_bf = []
+
+        def turn_back(blk):
+            words = c_t[blk][:].rearrange("t u p e -> t (u p e)").bitcast(F32)
+            back = psum.tile([P, 2, P], F32, name="back", tag="bank", bufs=5)
+            for u in range(2):
+                nc.tensor.transpose(back[:, u, :], words[:, u * P : (u + 1) * P], ident[:])
+            c = keep.tile([P, P * PACK], BF16, name=f"c_bf{blk}", align_bytes=64)
+            nc.scalar.copy(out=c[:].bitcast(F32).rearrange("p (t u) -> p t u", u=2), in_=back[:].rearrange("p u t -> p t u"))
+            c_bf.append(c)
+
+        for blk in range(BLOCKS):
+            prods = gated(3, P * blk, P * (blk + 1), every, f"prod3_{blk}")
+            if blk > 0:
+                turn_back(blk - 1)
+            round_sums(3, [blk], turn_and_add(prods, [blk]))
+        turn_back(BLOCKS - 1)
+
+        wp_codes = keep.tile([P, M], U32, name="wp_codes", tag="gate_sb", align_bytes=64)
         wp_scales = keep.tile([P, M], U8, name="wp_scales", align_bytes=64)
         for f0, f1 in ((0, 256), (256, M)):
             quantize(wp_codes[:, f0:f1], wp_scales[:, f0:f1], wp_bf[:, f0:f1, :].rearrange("p c t -> p (c t)"))
 
         out_rows = out.rearrange("(a p) t -> p a t", p=P)
-
-        def project(ci):
-            a, b = TOKEN_CHUNKS[ci]
-            nblk = (b - a) // P
-            words = c_t[ci][:].rearrange("t b u p e -> t (b u p e)").bitcast(F32)
-            back = psum.tile([P, nblk, 2, P], F32, name="back", tag="bank", bufs=5)
-            for blk in range(nblk):
-                for u in range(2):
-                    w0 = (2 * blk + u) * P
-                    nc.tensor.transpose(back[:, blk, u, :], words[:, w0 : w0 + P], ident[:])
-            c_bf = keep.tile([P, (b - a) * PACK], BF16, name=f"c_bf{a}", align_bytes=64)
-            nc.scalar.copy(
-                out=c_bf[:].bitcast(F32).rearrange("p (b t u) -> p b t u", b=nblk, u=2),
-                in_=back[:].rearrange("p b u t -> p b t u"),
-            )
-            c_codes = keep.tile([P, b - a], U32, name=f"c_codes{a}", align_bytes=64)
-            c_scales = keep.tile([P, b - a], U8, name=f"c_scales{a}", align_bytes=64)
-            quantize(c_codes[:], c_scales[:], c_bf[:])
-            res = keep.tile([P, M // P, b - a], F32, name=f"res{a}")
-            per_bank = 512 // (b - a)
-            for f0 in range(0, M // P, per_bank):
-                f1 = min(M // P, f0 + per_bank)
-                acc = psum.tile([P, f1 - f0, b - a], F32, name="acc", tag="bank", bufs=5)
-                for f in range(f0, f1):
+        for blk in range(BLOCKS):
+            c_codes = keep.tile([P, P], U32, name=f"c_codes{blk}", align_bytes=64)
+            c_scales = keep.tile([P, P], U8, name=f"c_scales{blk}", align_bytes=64)
+            quantize(c_codes[:], c_scales[:], c_bf[blk][:])
+            last = blk == BLOCKS - 1
+            groups = [[f] for f in range(M // P)] if last else [list(range(M // P))]
+            for g, fs in enumerate(groups):
+                acc = psum.tile([P, len(fs), P], F32, name="acc", tag="bank", bufs=5)
+                for s, f in enumerate(fs):
                     nc.tensor.matmul_mx(
-                        out=acc[:, f - f0, :],
+                        out=acc[:, s, :],
                         lhsT=wp_codes[:, P * f : P * (f + 1)].bitcast(FP8X4),
                         lhsT_scale=wp_scales[:, P * f : P * (f + 1)],
                         rhs=c_codes[:].bitcast(FP8X4),
@@ -230,11 +245,7 @@ def tile_moe_nxt_lin_none_kernel(tc, xT, w, wp, gate, offs, pos1, pos2, pos3, po
                         start=True,
                         stop=True,
                     )
-                nc.vector.tensor_copy(out=res[:, f0:f1, :], in_=acc[:])
-            nc.sync.dma_start(out=out_rows[:, :, a:b], in_=res[:])
-
-        for ci, (a, b) in enumerate(TOKEN_CHUNKS):
-            round_sums(3, a, b, combine(3, a, b, f"prod_late3_{a}"))
-            if ci > 0:
-                project(ci - 1)
-        project(len(TOKEN_CHUNKS) - 1)
+                res = keep.tile([P, len(fs), P], F32, name=f"res{blk}_{g}")
+                copy = nc.vector.tensor_copy if last and g != 1 else nc.scalar.copy
+                copy(out=res[:], in_=acc[:])
+                nc.sync.dma_start(out=out_rows[:, fs[0] : fs[-1] + 1, P * blk : P * (blk + 1)], in_=res[:])

@@ -21,11 +21,11 @@ P = 128
 PACK = 4
 PAIR = 2 * C
 PAIRS = E // 2
-WINDOW = 1408
-RUN = 1024
+WORD_WINDOW = 1408
+BYTE_WINDOW = 2048
 LIST_COL = 16
 BLOCKS = T // P
-X_PIECES = ((0, 256), (256, 384), (384, 512))
+X_PIECES = ((0, 128), (128, 256), (256, 384), (384, 512))
 
 
 def interleave(engine_copy, dst, src):
@@ -75,13 +75,13 @@ def tile_moe_nxt_lin_none_kernel(tc, xT, w, wp, gate, offs, pos1, pos2, pos3, po
         nc.sync.dma_start(out=wp_raw[:], in_=wp.rearrange("(p j) f -> p j f", j=PACK))
 
         ident = keep.tile([P, P], F32, name="ident")
-        x_codes = keep.tile([P, WINDOW], U32, name="x_codes", align_bytes=64)
-        x_scales = keep.tile([P, WINDOW], U8, name="x_scales", align_bytes=64)
+        x_codes = keep.tile([P, WORD_WINDOW], U32, name="x_codes", align_bytes=64)
+        x_scales = keep.tile([P, BYTE_WINDOW], U8, name="x_scales", align_bytes=64)
         nc.vector.memset(x_scales[:].bitcast(I32), 0)
-        nc.vector.memset(x_codes[:, T:WINDOW].bitcast(I32), 0)
+        nc.vector.memset(x_codes[:, T:WORD_WINDOW].bitcast(I32), 0)
         make_identity(nc, ident[:])
 
-        for (a, b), raw, copy in zip(X_PIECES, x_raw, (nc.vector.tensor_copy, nc.scalar.copy, nc.vector.tensor_copy)):
+        for (a, b), raw, copy in zip(X_PIECES, x_raw, (nc.vector.tensor_copy, nc.vector.tensor_copy, nc.scalar.copy, nc.vector.tensor_copy)):
             x_bf = keep.tile([P, b - a, PACK], BF16, name=f"x_bf{a}", align_bytes=64)
             interleave(copy, x_bf[:], raw[:])
             quantize(x_codes[:, a:b], x_scales[:, a:b], x_bf[:].rearrange("p c t -> p (c t)"))
@@ -89,16 +89,17 @@ def tile_moe_nxt_lin_none_kernel(tc, xT, w, wp, gate, offs, pos1, pos2, pos3, po
         y = {}
         slot_codes, slot_scales = [], []
 
-        def gather(window, i, dtype, name, tag):
-            got = keep.tile([P, RUN], dtype, name=name, tag=tag, align_bytes=64)
-            lst = offs_sb[:, i * RUN // LIST_COL : (i + 1) * RUN // LIST_COL]
+        def gather(window, i0, i1, dtype, name, tag):
+            got = keep.tile([P, (i1 - i0) * PAIR], dtype, name=name, tag=tag, align_bytes=64)
+            lst = offs_sb[:, i0 * PAIR // LIST_COL : i1 * PAIR // LIST_COL]
             nc.vector.tensor_copy(got[:], window[:].indirect(lst))
-            return [got[:, PAIR * h : PAIR * (h + 1)] for h in range(RUN // PAIR)]
+            return [got[:, PAIR * h : PAIR * (h + 1)] for h in range(i1 - i0)]
 
         wq = {}
 
         def quant_w(j, e0, g, n):
-            cw = keep.tile([P, n * P], U32, name=f"w_codes{j}_{e0}", align_bytes=64)
+            tag = "w_bf2_0" if (j, e0) == (0, E - 2) else f"w_codes{j}_{e0}"
+            cw = keep.tile([P, n * P], U32, name=f"w_codes{j}_{e0}", tag=tag, align_bytes=64)
             cs = keep.tile([P, n * P], U8, name=f"w_scales{j}_{e0}", align_bytes=64)
             quantize(cw[:], cs[:], g[:].rearrange("p s c t -> p (s c t)"))
             for s in range(n):
@@ -155,9 +156,9 @@ def tile_moe_nxt_lin_none_kernel(tc, xT, w, wp, gate, offs, pos1, pos2, pos3, po
                     in_=sums[:, s, :].rearrange("t (p u e) -> t u p e", u=2, e=2),
                 )
 
-        slot_codes += gather(x_codes, 0, U32, "slot_codes0", "slot_codes0")
-        slot_scales += gather(x_scales, 0, U8, "slot_scales0", "slot_scales0")
-        slot_codes += gather(x_codes, 1, U32, "slot_codes1", "slot_codes1")
+        slot_codes += gather(x_codes, 0, 2, U32, "slot_codes0", "slot_codes0")
+        slot_scales += gather(x_scales, 0, 3, U8, "slot_scales0", "slot_scales0")
+        slot_codes += gather(x_codes, 2, 4, U32, "slot_codes1", "slot_codes1")
         g1 = staging(1, 0, E)
         for i in range(PAIRS):
             g0 = staging(0, 2 * i, 2)
@@ -165,8 +166,7 @@ def tile_moe_nxt_lin_none_kernel(tc, xT, w, wp, gate, offs, pos1, pos2, pos3, po
                 interleave(nc.scalar.copy, g0[:, s], w_t0[2 * i + s])
                 interleave(nc.scalar.copy, g1[:, 2 * i + s], w_t1[2 * i + s])
             quant_w(0, 2 * i, g0, 2)
-            if i == 1:
-                slot_scales += gather(x_scales, 1, U8, "slot_scales1", "w_bf0_2")
+        slot_scales += gather(x_scales, 3, 4, U8, "slot_scales1", "w_bf0_6")
         quant_w(1, 0, g1, E)
         y[0] = keep.tile([P, SLOTS], F32, name="y0", tag=f"w_raw{E - 1}_0", align_bytes=64)
         for j in range(1, 4):
@@ -178,20 +178,23 @@ def tile_moe_nxt_lin_none_kernel(tc, xT, w, wp, gate, offs, pos1, pos2, pos3, po
         held = [turn_and_add(gated(0, 0, T, every, "prod0"), every)]
 
         def upper(j, raws):
-            g = staging(j, 0, E)
-            for e in range(E):
-                interleave(nc.scalar.copy, g[:, e], raws[e][:])
-            quant_w(j, 0, g, E)
+            for e0 in (0, E // 2):
+                g = staging(j, e0, E // 2)
+                for s in range(E // 2):
+                    interleave(nc.scalar.copy, g[:, s], raws[e0 + s][:])
+                quant_w(j, e0, g, E // 2)
             for i in range(PAIRS):
                 experts(j, i)
 
         upper(2, w_t2)
-        prods = gated(1, 0, T, [0, 1], "prod1")
-        prods.update(gated(1, 0, T, [2, 3], "w_bf2_0"))
+        prods = gated(1, 0, T, [0], "prod1")
+        prods.update(gated(1, 0, T, [1], "w_bf2_0"))
+        prods.update(gated(1, 0, T, [2, 3], "w_bf2_4"))
         held.append(turn_and_add(prods, every))
         upper(3, w_t3)
-        prods = gated(2, 0, T // 2, every, "prod2")
-        prods.update(gated(2, T // 2, T, every, "w_bf3_0"))
+        prods = gated(2, 0, T, [0], "prod2")
+        prods.update(gated(2, 0, T, [1], "w_bf3_0"))
+        prods.update(gated(2, 0, T, [2, 3], "w_bf3_4"))
         held.append(turn_and_add(prods, every))
         c_t = [
             keep.tile([P, 2, P, 2], BF16, name=f"c_t{blk}", tag=f"w_raw{E - BLOCKS + blk}_384", align_bytes=64)
@@ -214,11 +217,14 @@ def tile_moe_nxt_lin_none_kernel(tc, xT, w, wp, gate, offs, pos1, pos2, pos3, po
             nc.scalar.copy(out=c[:].bitcast(F32).rearrange("p (t u) -> p t u", u=2), in_=back[:].rearrange("p u t -> p t u"))
             c_bf.append(c)
 
-        for blk in range(BLOCKS):
-            prods = gated(3, P * blk, P * (blk + 1), every, f"prod3_{blk}")
-            if blk > 0:
-                turn_back(blk - 1)
-            round_sums(3, [blk], turn_and_add(prods, [blk]))
+        done = []
+        for blocks in ([0, 1], [2], [3]):
+            prods = gated(3, P * blocks[0], P * (blocks[-1] + 1), every, f"prod3_{blocks[0]}")
+            for blk in done:
+                turn_back(blk)
+            for blk in blocks:
+                round_sums(3, [blk], turn_and_add(prods, [blk]))
+            done = blocks
         turn_back(BLOCKS - 1)
 
         wp_codes = keep.tile([P, M], U32, name="wp_codes", tag="gate_sb", align_bytes=64)

@@ -30,8 +30,8 @@ X_PIECES = ((0, 128), (128, 256), (256, 384), (384, 512))
 
 def interleave(engine_copy, dst, src):
     engine_copy(
-        out=dst.rearrange("p (c i) t -> p c t i", i=4),
-        in_=src.rearrange("p t (c i) -> p c t i", i=4),
+        out=dst.rearrange("p (c i) t -> p c t i", i=2),
+        in_=src.rearrange("p t (c i) -> p c t i", i=2),
     )
 
 

@@ -19,239 +19,262 @@ MULT = mybir.AluOpType.mult
 
 P = 128
 PACK = 4
+ALIGN = 64
+LIST_COL = 16
 PAIR = 2 * C
 PAIRS = E // 2
+HALF = E // 2
+BLOCKS = T // P
+BANKS = 4
 WORD_WINDOW = 1408
 BYTE_WINDOW = 2048
-LIST_COL = 16
-BLOCKS = T // P
-X_PIECES = ((0, 128), (128, 256), (256, 384), (384, 512))
+X_PIECES = ((0, 256), (256, 384), (384, 512))
+LAST_TILE_GROUPS = ((0, 1), (2,), (3,))
+WP_CALLS = ((0, 256), (256, M))
 
 
-def interleave(engine_copy, dst, src):
-    engine_copy(
-        out=dst.rearrange("p (c i) t -> p c t i", i=2),
-        in_=src.rearrange("p t (c i) -> p c t i", i=2),
-    )
+def interleave(copy, dst, src):
+    copy(out=dst.rearrange("p (c i) t -> p c t i", i=2), in_=src.rearrange("p t (c i) -> p c t i", i=2))
 
 
 def tile_moe_nxt_lin_none_kernel(tc, xT, w, wp, gate, offs, pos1, pos2, pos3, pos4, out):
     nc = tc.nc
     with ExitStack() as ctx:
         keep = ctx.enter_context(tc.tile_pool(name="keep", bufs=1))
-        psum = ctx.enter_context(tc.psum_pool(name="psum", bufs=1))
+        psum = ctx.enter_context(tc.psum_pool(name="psum", bufs=BANKS))
+
+        def sbuf(shape, dtype, name, reuses=None):
+            return keep.tile(shape, dtype, name=name, tag=reuses or name, align_bytes=ALIGN)
 
         def quantize(codes, scales, grouped):
             nc.vector.quantize_mx(out=codes.bitcast(FP8X4), scales=scales, in_=grouped)
 
-        x_rows = xT.rearrange("(p j) t -> p j t", j=PACK)
-        x_raw = []
-        for a, b in X_PIECES:
-            t = keep.tile([P, PACK, b - a], F32, name=f"x_raw{a}")
-            nc.sync.dma_start(out=t[:], in_=x_rows[:, :, a:b])
-            x_raw.append(t)
-        offs_sb = keep.tile([P, SLOTS // LIST_COL], U16, name="offs_sb")
-        nc.sync.dma_start(offs_sb[:], offs)
+        def matmul_mx(acc, lhs, rhs):
+            nc.tensor.matmul_mx(
+                out=acc,
+                lhsT=lhs[0].bitcast(FP8X4),
+                lhsT_scale=lhs[1],
+                rhs=rhs[0].bitcast(FP8X4),
+                rhs_scale=rhs[1],
+                start=True,
+                stop=True,
+            )
 
-        def load_w(e, c0, c1):
-            t = keep.tile([P, PACK, c1 - c0], F32, name=f"w_raw{e}_{c0}", tag=f"w_raw{e}_{c0}", align_bytes=64)
-            nc.sync.dma_start(out=t[:], in_=w[e].rearrange("(p j) n -> p j n", j=PACK)[:, :, c0:c1])
-            return t
+        def load_rows(matrix, c0, c1, name):
+            raw = sbuf([P, PACK, c1 - c0], F32, name)
+            nc.sync.dma_start(out=raw[:], in_=matrix.rearrange("(p j) c -> p j c", j=PACK)[:, :, c0:c1])
+            return raw
 
-        first = [load_w(0, 0, P), load_w(0, P, 2 * P)]
-        rest = [load_w(e, 0, 2 * P) for e in range(1, E)]
-        w_t0 = [first[0][:]] + [t[:, :, 0:P] for t in rest]
-        w_t1 = [first[1][:]] + [t[:, :, P : 2 * P] for t in rest]
-        pos_sb = []
-        for r, pos in enumerate((pos1, pos2, pos3, pos4)):
-            t = keep.tile([P, T // LIST_COL], U16, name=f"pos_sb{r}")
-            nc.sync.dma_start(t[:], pos)
-            pos_sb.append(t)
-        gate_sb = keep.tile([P, TOP, T], F32, name="gate_sb", tag="gate_sb", align_bytes=64)
-        nc.sync.dma_start(out=gate_sb[:], in_=gate[:, 0:P, :].rearrange("r p t -> p r t"))
-        w_t2 = [load_w(e, 256, 384) for e in range(E)]
-        w_t3 = [load_w(e, 384, 512) for e in range(E)]
-        wp_raw = keep.tile([P, PACK, M], F32, name="wp_raw")
-        nc.sync.dma_start(out=wp_raw[:], in_=wp.rearrange("(p j) f -> p j f", j=PACK))
+        def load_list(entries, name):
+            tile = keep.tile(list(entries.shape), U16, name=name)
+            nc.sync.dma_start(tile[:], entries)
+            return tile
+
+        w_raw = {}
+
+        def load_w(e, j0, j1):
+            raw = load_rows(w[e], P * j0, P * j1, f"w_raw{e}_{j0}")
+            for j in range(j0, j1):
+                w_raw[(j, e)] = raw[:, :, P * (j - j0) : P * (j - j0 + 1)]
+
+        gate_sb = []
+
+        def load_gate(r):
+            tile = sbuf([P, T], F32, f"gate{r}")
+            nc.sync.dma_start(out=tile[:], in_=gate[r, 0:P, :])
+            gate_sb.append(tile)
+
+        x_raw = [load_rows(xT, a, b, f"x_raw{a}") for a, b in X_PIECES]
+        offs_sb = load_list(offs, "offs_sb")
+        load_w(0, 0, 1)
+        load_w(0, 1, 2)
+        for e in range(1, E):
+            load_w(e, 0, 2)
+        pos_sb = [load_list(pos, f"pos_sb{r}") for r, pos in enumerate((pos1, pos2, pos3, pos4))]
+        for e in range(HALF):
+            load_gate(e)
+            load_w(e, 2, 4)
+        for j in (2, 3):
+            for e in range(HALF, E):
+                load_w(e, j, j + 1)
+        wp_raw = load_rows(wp, 0, M, "wp_raw")
 
         ident = keep.tile([P, P], F32, name="ident")
-        x_codes = keep.tile([P, WORD_WINDOW], U32, name="x_codes", align_bytes=64)
-        x_scales = keep.tile([P, BYTE_WINDOW], U8, name="x_scales", align_bytes=64)
-        nc.vector.memset(x_scales[:].bitcast(I32), 0)
-        nc.vector.memset(x_codes[:, T:WORD_WINDOW].bitcast(I32), 0)
         make_identity(nc, ident[:])
 
-        for (a, b), raw, copy in zip(X_PIECES, x_raw, (nc.vector.tensor_copy, nc.vector.tensor_copy, nc.scalar.copy, nc.vector.tensor_copy)):
-            x_bf = keep.tile([P, b - a, PACK], BF16, name=f"x_bf{a}", align_bytes=64)
+        x_codes = sbuf([P, WORD_WINDOW], U32, "x_codes")
+        x_scales = sbuf([P, BYTE_WINDOW], U8, "x_scales")
+        nc.vector.memset(x_scales[:].bitcast(I32), 0)
+        nc.vector.memset(x_codes[:, T:WORD_WINDOW].bitcast(I32), 0)
+        x_copies = (nc.vector.tensor_copy, nc.scalar.copy, nc.vector.tensor_copy)
+        for (a, b), raw, copy in zip(X_PIECES, x_raw, x_copies):
+            x_bf = sbuf([P, b - a, PACK], BF16, f"x_bf{a}")
             interleave(copy, x_bf[:], raw[:])
             quantize(x_codes[:, a:b], x_scales[:, a:b], x_bf[:].rearrange("p c t -> p (c t)"))
 
-        y = {}
-        slot_codes, slot_scales = [], []
-
-        def gather(window, i0, i1, dtype, name, tag):
-            got = keep.tile([P, (i1 - i0) * PAIR], dtype, name=name, tag=tag, align_bytes=64)
-            lst = offs_sb[:, i0 * PAIR // LIST_COL : i1 * PAIR // LIST_COL]
-            nc.vector.tensor_copy(got[:], window[:].indirect(lst))
+        def gather_slots(window, i0, i1, name, reuses=None):
+            got = sbuf([P, (i1 - i0) * PAIR], window.dtype, name, reuses)
+            entries = offs_sb[:, i0 * PAIR // LIST_COL : i1 * PAIR // LIST_COL]
+            nc.vector.tensor_copy(got[:], window[:].indirect(entries))
             return [got[:, PAIR * h : PAIR * (h + 1)] for h in range(i1 - i0)]
 
-        wq = {}
+        w_mx = {}
 
-        def quant_w(j, e0, g, n):
-            tag = "w_bf2_0" if (j, e0) == (0, E - 2) else f"w_codes{j}_{e0}"
-            cw = keep.tile([P, n * P], U32, name=f"w_codes{j}_{e0}", tag=tag, align_bytes=64)
-            cs = keep.tile([P, n * P], U8, name=f"w_scales{j}_{e0}", align_bytes=64)
-            quantize(cw[:], cs[:], g[:].rearrange("p s c t -> p (s c t)"))
-            for s in range(n):
-                wq[(j, e0 + s)] = (cw[:, P * s : P * (s + 1)], cs[:, P * s : P * (s + 1)])
+        def staging(j, e0, count):
+            return sbuf([P, count, P, PACK], BF16, f"w_bf{j}_{e0}")
 
-        def staging(j, e0, n):
-            return keep.tile([P, n, P, PACK], BF16, name=f"w_bf{j}_{e0}", tag=f"w_bf{j}_{e0}", align_bytes=64)
+        def quantize_w(j, e0, staged, reuses=None):
+            count = staged.shape[1]
+            codes = sbuf([P, count * P], U32, f"w_codes{j}_{e0}", reuses)
+            scales = sbuf([P, count * P], U8, f"w_scales{j}_{e0}")
+            quantize(codes[:], scales[:], staged[:].rearrange("p s c t -> p (s c t)"))
+            for s in range(count):
+                w_mx[(j, e0 + s)] = (codes[:, P * s : P * (s + 1)], scales[:, P * s : P * (s + 1)])
 
-        def experts(j, i):
-            bank = psum.tile([P, PAIR], F32, name="bank", tag="bank", bufs=5)
-            for s in range(2):
-                cw, cs = wq[(j, 2 * i + s)]
-                cols = slice(C * s, C * (s + 1))
-                nc.tensor.matmul_mx(
-                    out=bank[:, cols],
-                    lhsT=cw.bitcast(FP8X4),
-                    lhsT_scale=cs,
-                    rhs=slot_codes[i][:, cols].bitcast(FP8X4),
-                    rhs_scale=slot_scales[i][:, cols],
-                    start=True,
-                    stop=True,
-                )
-            nc.scalar.copy(out=y[j][:, PAIR * i : PAIR * (i + 1)], in_=bank[:])
+        def experts(j):
+            for i in range(PAIRS):
+                bank = psum.tile([P, PAIR], F32, name="bank", tag="products")
+                for s in range(2):
+                    cols = slice(C * s, C * (s + 1))
+                    matmul_mx(bank[:, cols], w_mx[(j, 2 * i + s)], (slot_codes[i][:, cols], slot_scales[i][:, cols]))
+                nc.scalar.copy(out=y[j][:, PAIR * i : PAIR * (i + 1)], in_=bank[:])
 
-        def gated(j, a, b, rs, tag):
-            prod = keep.tile([P, len(rs), b - a], F32, name=f"prod{j}_{a}_{rs[0]}", tag=tag, align_bytes=64)
-            for s, r in enumerate(rs):
-                nc.vector.tensor_tensor(
-                    prod[:, s, :],
-                    y[j][:].indirect(pos_sb[r][:, a // LIST_COL : b // LIST_COL]),
-                    gate_sb[:, r, a:b],
-                    MULT,
-                )
-            return {(r, a // P + blk): prod[:, s, P * blk : P * (blk + 1)] for s, r in enumerate(rs) for blk in range((b - a) // P)}
+        def gated(j, a, b, choices, dst):
+            views = {}
+            for s, r in enumerate(choices):
+                entries = pos_sb[r][:, a // LIST_COL : b // LIST_COL]
+                nc.vector.tensor_tensor(dst[:, s, :], y[j][:].indirect(entries), gate_sb[r][:, a:b], MULT)
+                for blk in range(a // P, b // P):
+                    views[(r, blk)] = dst[:, s, P * blk - a : P * (blk + 1) - a]
+            return views
 
-        def turn_and_add(prods, blocks):
-            sums = psum.tile([P, len(blocks), P], F32, name="sums", tag="sums", bufs=3)
+        def turn_and_add(sums, product, r):
+            nc.tensor.matmul(
+                out=sums, lhsT=product, rhs=ident[:], start=(r == 0), stop=(r == TOP - 1), is_transpose=True
+            )
+
+        def sum_blocks(products, blocks):
+            sums = psum.tile([P, len(blocks), P], F32, name="sums", tag="sums")
             for s, blk in enumerate(blocks):
                 for r in range(TOP):
-                    nc.tensor.matmul(
-                        out=sums[:, s, :],
-                        lhsT=prods[(r, blk)],
-                        rhs=ident[:],
-                        start=(r == 0),
-                        stop=(r == TOP - 1),
-                        is_transpose=True,
-                    )
-            return sums
+                    turn_and_add(sums[:, s, :], products[(r, blk)], r)
+            return {blk: sums[:, s, :] for s, blk in enumerate(blocks)}
 
-        def round_sums(j, blocks, sums):
-            for s, blk in enumerate(blocks):
+        slot_codes = gather_slots(x_codes, 0, 2, "slot_codes0")
+        slot_scales = gather_slots(x_scales, 0, PAIRS - 1, "slot_scales0")
+        slot_codes += gather_slots(x_codes, 2, PAIRS, "slot_codes1")
+        staged1 = staging(1, 0, E)
+        for i in range(PAIRS):
+            staged0 = staging(0, 2 * i, 2)
+            for s in range(2):
+                interleave(nc.scalar.copy, staged0[:, s], w_raw[(0, 2 * i + s)])
+                interleave(nc.scalar.copy, staged1[:, 2 * i + s], w_raw[(1, 2 * i + s)])
+            quantize_w(0, 2 * i, staged0, "w_bf2_0" if i == PAIRS - 1 else None)
+        slot_scales += gather_slots(x_scales, PAIRS - 1, PAIRS, "slot_scales1", f"w_bf0_{E - 2}")
+        quantize_w(1, 0, staged1)
+        y = [sbuf([P, SLOTS], F32, "y0", f"w_raw{E - 1}_0")] + [sbuf([P, SLOTS], F32, f"y{j}") for j in range(1, 4)]
+        experts(0)
+        experts(1)
+
+        all_blocks = range(BLOCKS)
+        all_choices = range(TOP)
+        c_sums = [sum_blocks(gated(0, 0, T, all_choices, sbuf([P, TOP, T], F32, "prod0")), all_blocks)]
+
+        def upper_tile(j, reuses=None):
+            for e0 in (0, HALF):
+                staged = staging(j, e0, HALF)
+                for s in range(HALF):
+                    interleave(nc.scalar.copy, staged[:, s], w_raw[(j, e0 + s)])
+                quantize_w(j, e0, staged, reuses if e0 == 0 else None)
+            experts(j)
+
+        def first_two_choices(j):
+            products = gated(j, 0, T, [0], sbuf([P, 1, T], F32, f"prod{j}_0"))
+            products.update(gated(j, 0, T, [1], sbuf([P, 1, T], F32, f"prod{j}_1", f"w_bf{j + 1}_0")))
+            return products
+
+        upper_tile(2)
+        products = first_two_choices(1)
+        products.update(gated(1, 0, T, [2, 3], sbuf([P, 2, T], F32, "prod1_2", f"w_bf2_{HALF}")))
+        c_sums.append(sum_blocks(products, all_blocks))
+
+        upper_tile(3, "y1")
+        products = first_two_choices(2)
+        late = sbuf([P, 2, T], F32, "prod2_2", f"w_bf3_{HALF}")
+        products.update(gated(2, 0, T, [2], late[:, 0:1, :]))
+        for a, b in ((0, T // 2), (T // 2, T)):
+            products.update(gated(2, a, b, [3], late[:, 1:2, a:b]))
+        two_banks = [psum.tile([P, 2, P], F32, name="sums", tag="sums") for h in range(2)]
+        for s in range(2):
+            for r in all_choices:
+                for h in range(2):
+                    turn_and_add(two_banks[h][:, s, :], products[(r, 2 * s + h)], r)
+        c_sums.append({2 * s + h: two_banks[h][:, s, :] for h in range(2) for s in range(2)})
+
+        c_rows = [sbuf([P, 2, P, 2], BF16, f"c_rows{blk}", f"w_raw{HALF + blk}_3") for blk in all_blocks]
+
+        def round_sums(j, sums):
+            for blk in sums:
                 nc.scalar.copy(
-                    out=c_t[blk][:, :, 32 * j : 32 * (j + 1), :],
-                    in_=sums[:, s, :].rearrange("t (p u e) -> t u p e", u=2, e=2),
+                    out=c_rows[blk][:, :, 32 * j : 32 * (j + 1), :],
+                    in_=sums[blk].rearrange("t (p u i) -> t u p i", u=2, i=2),
                 )
 
-        slot_codes += gather(x_codes, 0, 2, U32, "slot_codes0", "slot_codes0")
-        slot_scales += gather(x_scales, 0, 3, U8, "slot_scales0", "slot_scales0")
-        slot_codes += gather(x_codes, 2, 4, U32, "slot_codes1", "slot_codes1")
-        g1 = staging(1, 0, E)
-        for i in range(PAIRS):
-            g0 = staging(0, 2 * i, 2)
-            for s in range(2):
-                interleave(nc.scalar.copy, g0[:, s], w_t0[2 * i + s])
-                interleave(nc.scalar.copy, g1[:, 2 * i + s], w_t1[2 * i + s])
-            quant_w(0, 2 * i, g0, 2)
-        slot_scales += gather(x_scales, 3, 4, U8, "slot_scales1", "w_bf0_6")
-        quant_w(1, 0, g1, E)
-        y[0] = keep.tile([P, SLOTS], F32, name="y0", tag=f"w_raw{E - 1}_0", align_bytes=64)
-        for j in range(1, 4):
-            y[j] = keep.tile([P, SLOTS], F32, name=f"y{j}")
-        for j in range(2):
-            for i in range(PAIRS):
-                experts(j, i)
-        every = list(range(BLOCKS))
-        held = [turn_and_add(gated(0, 0, T, every, "prod0"), every)]
+        for j, sums in enumerate(c_sums):
+            round_sums(j, sums)
 
-        def upper(j, raws):
-            for e0 in (0, E // 2):
-                g = staging(j, e0, E // 2)
-                for s in range(E // 2):
-                    interleave(nc.scalar.copy, g[:, s], raws[e0 + s][:])
-                quant_w(j, e0, g, E // 2)
-            for i in range(PAIRS):
-                experts(j, i)
-
-        upper(2, w_t2)
-        prods = gated(1, 0, T, [0], "prod1")
-        prods.update(gated(1, 0, T, [1], "w_bf2_0"))
-        prods.update(gated(1, 0, T, [2, 3], "w_bf2_4"))
-        held.append(turn_and_add(prods, every))
-        upper(3, w_t3)
-        prods = gated(2, 0, T, [0], "prod2")
-        prods.update(gated(2, 0, T, [1], "w_bf3_0"))
-        prods.update(gated(2, 0, T, [2, 3], "w_bf3_4"))
-        held.append(turn_and_add(prods, every))
-        c_t = [
-            keep.tile([P, 2, P, 2], BF16, name=f"c_t{blk}", tag=f"w_raw{E - BLOCKS + blk}_384", align_bytes=64)
-            for blk in range(BLOCKS)
-        ]
-        for j in range(3):
-            round_sums(j, every, held[j])
-
-        wp_bf = keep.tile([P, M, PACK], BF16, name="wp_bf", tag="slot_codes1", align_bytes=64)
+        wp_bf = sbuf([P, M, PACK], BF16, "wp_bf", "slot_codes1")
         interleave(nc.scalar.copy, wp_bf[:], wp_raw[:])
 
         c_bf = []
 
         def turn_back(blk):
-            words = c_t[blk][:].rearrange("t u p e -> t (u p e)").bitcast(F32)
-            back = psum.tile([P, 2, P], F32, name="back", tag="bank", bufs=5)
+            words = c_rows[blk][:].rearrange("t u p i -> t (u p i)").bitcast(F32)
+            back = psum.tile([P, 2, P], F32, name="back", tag="products")
             for u in range(2):
                 nc.tensor.transpose(back[:, u, :], words[:, u * P : (u + 1) * P], ident[:])
-            c = keep.tile([P, P * PACK], BF16, name=f"c_bf{blk}", align_bytes=64)
-            nc.scalar.copy(out=c[:].bitcast(F32).rearrange("p (t u) -> p t u", u=2), in_=back[:].rearrange("p u t -> p t u"))
-            c_bf.append(c)
+            grouped = sbuf([P, P * PACK], BF16, f"c_bf{blk}")
+            nc.scalar.copy(
+                out=grouped[:].bitcast(F32).rearrange("p (t u) -> p t u", u=2), in_=back[:].rearrange("p u t -> p t u")
+            )
+            c_bf.append(grouped)
 
-        done = []
-        for blocks in ([0, 1], [2], [3]):
-            prods = gated(3, P * blocks[0], P * (blocks[-1] + 1), every, f"prod3_{blocks[0]}")
-            for blk in done:
+        finished = ()
+        for blocks in LAST_TILE_GROUPS:
+            a, b = P * blocks[0], P * (blocks[-1] + 1)
+            products = gated(3, a, b, all_choices, sbuf([P, TOP, b - a], F32, f"prod3_{a}"))
+            for blk in finished:
                 turn_back(blk)
             for blk in blocks:
-                round_sums(3, [blk], turn_and_add(prods, [blk]))
-            done = blocks
-        turn_back(BLOCKS - 1)
+                round_sums(3, sum_blocks(products, [blk]))
+            finished = blocks
+        for blk in finished:
+            turn_back(blk)
 
-        wp_codes = keep.tile([P, M], U32, name="wp_codes", tag="gate_sb", align_bytes=64)
-        wp_scales = keep.tile([P, M], U8, name="wp_scales", align_bytes=64)
-        for f0, f1 in ((0, 256), (256, M)):
+        wp_codes = sbuf([P, M], U32, "wp_codes", f"gate{TOP - 1}")
+        wp_scales = sbuf([P, M], U8, "wp_scales")
+        for f0, f1 in WP_CALLS:
             quantize(wp_codes[:, f0:f1], wp_scales[:, f0:f1], wp_bf[:, f0:f1, :].rearrange("p c t -> p (c t)"))
 
         out_rows = out.rearrange("(a p) t -> p a t", p=P)
-        for blk in range(BLOCKS):
-            c_codes = keep.tile([P, P], U32, name=f"c_codes{blk}", align_bytes=64)
-            c_scales = keep.tile([P, P], U8, name=f"c_scales{blk}", align_bytes=64)
+        row_tiles = M // P
+
+        def project(blk, c_mx, f0, f1, tag, copy):
+            acc = psum.tile([P, f1 - f0, P], F32, name="acc", tag=tag)
+            for f in range(f0, f1):
+                cols = slice(P * f, P * (f + 1))
+                matmul_mx(acc[:, f - f0, :], (wp_codes[:, cols], wp_scales[:, cols]), c_mx)
+            result = keep.tile([P, f1 - f0, P], F32, name=f"result{blk}_{f0}")
+            copy(out=result[:], in_=acc[:])
+            nc.sync.dma_start(out=out_rows[:, f0:f1, P * blk : P * (blk + 1)], in_=result[:])
+
+        for blk in all_blocks:
+            c_codes = sbuf([P, P], U32, f"c_codes{blk}")
+            c_scales = sbuf([P, P], U8, f"c_scales{blk}")
             quantize(c_codes[:], c_scales[:], c_bf[blk][:])
-            last = blk == BLOCKS - 1
-            groups = [[f] for f in range(M // P)] if last else [list(range(M // P))]
-            for g, fs in enumerate(groups):
-                acc = psum.tile([P, len(fs), P], F32, name="acc", tag="bank", bufs=5)
-                for s, f in enumerate(fs):
-                    nc.tensor.matmul_mx(
-                        out=acc[:, s, :],
-                        lhsT=wp_codes[:, P * f : P * (f + 1)].bitcast(FP8X4),
-                        lhsT_scale=wp_scales[:, P * f : P * (f + 1)],
-                        rhs=c_codes[:].bitcast(FP8X4),
-                        rhs_scale=c_scales[:],
-                        start=True,
-                        stop=True,
-                    )
-                res = keep.tile([P, len(fs), P], F32, name=f"res{blk}_{g}")
-                copy = nc.vector.tensor_copy if last and g != 1 else nc.scalar.copy
-                copy(out=res[:], in_=acc[:])
-                nc.sync.dma_start(out=out_rows[:, fs[0] : fs[-1] + 1, P * blk : P * (blk + 1)], in_=res[:])
+            c_mx = (c_codes[:], c_scales[:])
+            if blk < BLOCKS - 1:
+                project(blk, c_mx, 0, row_tiles, "products", nc.scalar.copy)
+            else:
+                for f in range(row_tiles):
+                    project(blk, c_mx, f, f + 1, "sums", nc.scalar.copy if f % 2 else nc.vector.tensor_copy)

from contextlib import ExitStack

import concourse.mybir as mybir
from concourse.masks import make_identity

K, T, E, C, N, M = 512, 512, 8, 256, 512, 384
TOP = 4
SLOTS = E * C
FLOPS = 2 * K * N * SLOTS + 2 * N * M * T

F32 = mybir.dt.float32
BF16 = mybir.dt.bfloat16
I32 = mybir.dt.int32
U32 = mybir.dt.uint32
U16 = mybir.dt.uint16
U8 = mybir.dt.uint8
FP8X4 = mybir.dt.float8_e4m3fn_x4
MULT = mybir.AluOpType.mult

P = 128
PACK = 4
ALIGN = 64
LIST_COL = 16
PAIR = 2 * C
PAIRS = E // 2
HALF = E // 2
BLOCKS = T // P
BANKS = 4
WORD_WINDOW = 1408
BYTE_WINDOW = 2048
X_PIECES = ((0, 256), (256, 384), (384, 512))
LAST_TILE_GROUPS = ((0, 1), (2,), (3,))
WP_CALLS = ((0, 256), (256, M))


def interleave(copy, dst, src):
    copy(out=dst.rearrange("p (c i) t -> p c t i", i=2), in_=src.rearrange("p t (c i) -> p c t i", i=2))


def tile_moe_nxt_lin_none_kernel(tc, xT, w, wp, gate, offs, pos1, pos2, pos3, pos4, out):
    nc = tc.nc
    with ExitStack() as ctx:
        keep = ctx.enter_context(tc.tile_pool(name="keep", bufs=1))
        psum = ctx.enter_context(tc.psum_pool(name="psum", bufs=BANKS))

        def sbuf(shape, dtype, name, reuses=None):
            return keep.tile(shape, dtype, name=name, tag=reuses or name, align_bytes=ALIGN)

        def quantize(codes, scales, grouped):
            nc.vector.quantize_mx(out=codes.bitcast(FP8X4), scales=scales, in_=grouped)

        def matmul_mx(acc, lhs, rhs):
            nc.tensor.matmul_mx(
                out=acc,
                lhsT=lhs[0].bitcast(FP8X4),
                lhsT_scale=lhs[1],
                rhs=rhs[0].bitcast(FP8X4),
                rhs_scale=rhs[1],
                start=True,
                stop=True,
            )

        def load_rows(matrix, c0, c1, name):
            raw = sbuf([P, PACK, c1 - c0], F32, name)
            nc.sync.dma_start(out=raw[:], in_=matrix.rearrange("(p j) c -> p j c", j=PACK)[:, :, c0:c1])
            return raw

        def load_list(entries, name):
            tile = keep.tile(list(entries.shape), U16, name=name)
            nc.sync.dma_start(tile[:], entries)
            return tile

        w_raw = {}

        def load_w(e, j0, j1):
            raw = load_rows(w[e], P * j0, P * j1, f"w_raw{e}_{j0}")
            for j in range(j0, j1):
                w_raw[(j, e)] = raw[:, :, P * (j - j0) : P * (j - j0 + 1)]

        gate_sb = []

        def load_gate(r):
            tile = sbuf([P, T], F32, f"gate{r}")
            nc.sync.dma_start(out=tile[:], in_=gate[r, 0:P, :])
            gate_sb.append(tile)

        x_raw = [load_rows(xT, a, b, f"x_raw{a}") for a, b in X_PIECES]
        offs_sb = load_list(offs, "offs_sb")
        load_w(0, 0, 1)
        load_w(0, 1, 2)
        for e in range(1, E):
            load_w(e, 0, 2)
        pos_sb = [load_list(pos, f"pos_sb{r}") for r, pos in enumerate((pos1, pos2, pos3, pos4))]
        for e in range(HALF):
            load_gate(e)
            load_w(e, 2, 4)
        for j in (2, 3):
            for e in range(HALF, E):
                load_w(e, j, j + 1)
        wp_raw = load_rows(wp, 0, M, "wp_raw")

        ident = keep.tile([P, P], F32, name="ident")
        make_identity(nc, ident[:])

        x_codes = sbuf([P, WORD_WINDOW], U32, "x_codes")
        x_scales = sbuf([P, BYTE_WINDOW], U8, "x_scales")
        nc.vector.memset(x_scales[:].bitcast(I32), 0)
        nc.vector.memset(x_codes[:, T:WORD_WINDOW].bitcast(I32), 0)
        x_copies = (nc.vector.tensor_copy, nc.scalar.copy, nc.vector.tensor_copy)
        for (a, b), raw, copy in zip(X_PIECES, x_raw, x_copies):
            x_bf = sbuf([P, b - a, PACK], BF16, f"x_bf{a}")
            interleave(copy, x_bf[:], raw[:])
            quantize(x_codes[:, a:b], x_scales[:, a:b], x_bf[:].rearrange("p c t -> p (c t)"))

        def gather_slots(window, i0, i1, name, reuses=None):
            got = sbuf([P, (i1 - i0) * PAIR], window.dtype, name, reuses)
            entries = offs_sb[:, i0 * PAIR // LIST_COL : i1 * PAIR // LIST_COL]
            nc.vector.tensor_copy(got[:], window[:].indirect(entries))
            return [got[:, PAIR * h : PAIR * (h + 1)] for h in range(i1 - i0)]

        w_mx = {}

        def staging(j, e0, count):
            return sbuf([P, count, P, PACK], BF16, f"w_bf{j}_{e0}")

        def quantize_w(j, e0, staged, reuses=None):
            count = staged.shape[1]
            codes = sbuf([P, count * P], U32, f"w_codes{j}_{e0}", reuses)
            scales = sbuf([P, count * P], U8, f"w_scales{j}_{e0}")
            quantize(codes[:], scales[:], staged[:].rearrange("p s c t -> p (s c t)"))
            for s in range(count):
                w_mx[(j, e0 + s)] = (codes[:, P * s : P * (s + 1)], scales[:, P * s : P * (s + 1)])

        def experts(j):
            for i in range(PAIRS):
                bank = psum.tile([P, PAIR], F32, name="bank", tag="products")
                for s in range(2):
                    cols = slice(C * s, C * (s + 1))
                    matmul_mx(bank[:, cols], w_mx[(j, 2 * i + s)], (slot_codes[i][:, cols], slot_scales[i][:, cols]))
                nc.scalar.copy(out=y[j][:, PAIR * i : PAIR * (i + 1)], in_=bank[:])

        def gated(j, a, b, choices, dst):
            views = {}
            for s, r in enumerate(choices):
                entries = pos_sb[r][:, a // LIST_COL : b // LIST_COL]
                nc.vector.tensor_tensor(dst[:, s, :], y[j][:].indirect(entries), gate_sb[r][:, a:b], MULT)
                for blk in range(a // P, b // P):
                    views[(r, blk)] = dst[:, s, P * blk - a : P * (blk + 1) - a]
            return views

        def turn_and_add(sums, product, r):
            nc.tensor.matmul(
                out=sums, lhsT=product, rhs=ident[:], start=(r == 0), stop=(r == TOP - 1), is_transpose=True
            )

        def sum_blocks(products, blocks):
            sums = psum.tile([P, len(blocks), P], F32, name="sums", tag="sums")
            for s, blk in enumerate(blocks):
                for r in range(TOP):
                    turn_and_add(sums[:, s, :], products[(r, blk)], r)
            return {blk: sums[:, s, :] for s, blk in enumerate(blocks)}

        slot_codes = gather_slots(x_codes, 0, 2, "slot_codes0")
        slot_scales = gather_slots(x_scales, 0, PAIRS - 1, "slot_scales0")
        slot_codes += gather_slots(x_codes, 2, PAIRS, "slot_codes1")
        staged1 = staging(1, 0, E)
        for i in range(PAIRS):
            staged0 = staging(0, 2 * i, 2)
            for s in range(2):
                interleave(nc.scalar.copy, staged0[:, s], w_raw[(0, 2 * i + s)])
                interleave(nc.scalar.copy, staged1[:, 2 * i + s], w_raw[(1, 2 * i + s)])
            quantize_w(0, 2 * i, staged0, "w_bf2_0" if i == PAIRS - 1 else None)
        slot_scales += gather_slots(x_scales, PAIRS - 1, PAIRS, "slot_scales1", f"w_bf0_{E - 2}")
        quantize_w(1, 0, staged1)
        y = [sbuf([P, SLOTS], F32, "y0", f"w_raw{E - 1}_0")] + [sbuf([P, SLOTS], F32, f"y{j}") for j in range(1, 4)]
        experts(0)
        experts(1)

        all_blocks = range(BLOCKS)
        all_choices = range(TOP)
        c_sums = [sum_blocks(gated(0, 0, T, all_choices, sbuf([P, TOP, T], F32, "prod0")), all_blocks)]

        def upper_tile(j, reuses=None):
            for e0 in (0, HALF):
                staged = staging(j, e0, HALF)
                for s in range(HALF):
                    interleave(nc.scalar.copy, staged[:, s], w_raw[(j, e0 + s)])
                quantize_w(j, e0, staged, reuses if e0 == 0 else None)
            experts(j)

        def first_two_choices(j):
            products = gated(j, 0, T, [0], sbuf([P, 1, T], F32, f"prod{j}_0"))
            products.update(gated(j, 0, T, [1], sbuf([P, 1, T], F32, f"prod{j}_1", f"w_bf{j + 1}_0")))
            return products

        upper_tile(2)
        products = first_two_choices(1)
        products.update(gated(1, 0, T, [2, 3], sbuf([P, 2, T], F32, "prod1_2", f"w_bf2_{HALF}")))
        c_sums.append(sum_blocks(products, all_blocks))

        upper_tile(3, "y1")
        products = first_two_choices(2)
        late = sbuf([P, 2, T], F32, "prod2_2", f"w_bf3_{HALF}")
        products.update(gated(2, 0, T, [2], late[:, 0:1, :]))
        for a, b in ((0, T // 2), (T // 2, T)):
            products.update(gated(2, a, b, [3], late[:, 1:2, a:b]))
        two_banks = [psum.tile([P, 2, P], F32, name="sums", tag="sums") for h in range(2)]
        for s in range(2):
            for r in all_choices:
                for h in range(2):
                    turn_and_add(two_banks[h][:, s, :], products[(r, 2 * s + h)], r)
        c_sums.append({2 * s + h: two_banks[h][:, s, :] for h in range(2) for s in range(2)})

        c_rows = [sbuf([P, 2, P, 2], BF16, f"c_rows{blk}", f"w_raw{HALF + blk}_3") for blk in all_blocks]

        def round_sums(j, sums):
            for blk in sums:
                nc.scalar.copy(
                    out=c_rows[blk][:, :, 32 * j : 32 * (j + 1), :],
                    in_=sums[blk].rearrange("t (p u i) -> t u p i", u=2, i=2),
                )

        for j, sums in enumerate(c_sums):
            round_sums(j, sums)

        wp_bf = sbuf([P, M, PACK], BF16, "wp_bf", "slot_codes1")
        interleave(nc.scalar.copy, wp_bf[:], wp_raw[:])

        c_bf = []

        def turn_back(blk):
            words = c_rows[blk][:].rearrange("t u p i -> t (u p i)").bitcast(F32)
            back = psum.tile([P, 2, P], F32, name="back", tag="products")
            for u in range(2):
                nc.tensor.transpose(back[:, u, :], words[:, u * P : (u + 1) * P], ident[:])
            grouped = sbuf([P, P * PACK], BF16, f"c_bf{blk}")
            nc.scalar.copy(
                out=grouped[:].bitcast(F32).rearrange("p (t u) -> p t u", u=2), in_=back[:].rearrange("p u t -> p t u")
            )
            c_bf.append(grouped)

        finished = ()
        for blocks in LAST_TILE_GROUPS:
            a, b = P * blocks[0], P * (blocks[-1] + 1)
            products = gated(3, a, b, all_choices, sbuf([P, TOP, b - a], F32, f"prod3_{a}"))
            for blk in finished:
                turn_back(blk)
            for blk in blocks:
                round_sums(3, sum_blocks(products, [blk]))
            finished = blocks
        for blk in finished:
            turn_back(blk)

        wp_codes = sbuf([P, M], U32, "wp_codes", f"gate{TOP - 1}")
        wp_scales = sbuf([P, M], U8, "wp_scales")
        for f0, f1 in WP_CALLS:
            quantize(wp_codes[:, f0:f1], wp_scales[:, f0:f1], wp_bf[:, f0:f1, :].rearrange("p c t -> p (c t)"))

        out_rows = out.rearrange("(a p) t -> p a t", p=P)
        row_tiles = M // P

        def project(blk, c_mx, f0, f1, tag, copy):
            acc = psum.tile([P, f1 - f0, P], F32, name="acc", tag=tag)
            for f in range(f0, f1):
                cols = slice(P * f, P * (f + 1))
                matmul_mx(acc[:, f - f0, :], (wp_codes[:, cols], wp_scales[:, cols]), c_mx)
            result = keep.tile([P, f1 - f0, P], F32, name=f"result{blk}_{f0}")
            copy(out=result[:], in_=acc[:])
            nc.sync.dma_start(out=out_rows[:, f0:f1, P * blk : P * (blk + 1)], in_=result[:])

        for blk in all_blocks:
            c_codes = sbuf([P, P], U32, f"c_codes{blk}")
            c_scales = sbuf([P, P], U8, f"c_scales{blk}")
            quantize(c_codes[:], c_scales[:], c_bf[blk][:])
            c_mx = (c_codes[:], c_scales[:])
            if blk < BLOCKS - 1:
                project(blk, c_mx, 0, row_tiles, "products", nc.scalar.copy)
            else:
                for f in range(row_tiles):
                    project(blk, c_mx, f, f + 1, "sums", nc.scalar.copy if f % 2 else nc.vector.tensor_copy)
